import numpy as np
import ml_dtypes


def mxq(x, axis, fmt="e4m3"):
    dtype, down = {"e4m3": (ml_dtypes.float8_e4m3fn, 7), "e5m2": (ml_dtypes.float8_e5m2, 14)}[fmt]
    v = np.moveaxis(np.asarray(x, np.float32).astype(ml_dtypes.bfloat16).astype(np.float64), axis, -1)
    blocks = v.reshape(v.shape[:-1] + (-1, 32))
    amax = np.abs(blocks).max(-1, keepdims=True)
    byte = np.maximum(np.where(amax > 0, np.frexp(amax)[1] - 1 + 127, 0) - down, 1)
    scale = np.exp2(byte - 127.0)
    codes = (blocks / scale).astype(np.float32).astype(dtype).astype(np.float64)
    return np.moveaxis((codes * scale).reshape(v.shape), -1, axis)


WIDE = False


def mx_kscale(k):
    if not WIDE:
        return np.ones(k)
    levels = np.array([10, -10, 5, -5, 0])
    if k % 512:
        return np.exp2(np.random.permutation(np.resize(levels, k // 32))).repeat(32)
    a = np.empty((k // 512, 16))
    for p in range(k // 512):
        a[p, :8] = np.random.permutation(np.resize(levels, 8))
        for g in range(8):
            far = levels[np.abs(levels - a[p, g]) >= 10]
            a[p, g + 8] = far[np.random.randint(len(far))]
    return np.exp2(a.ravel()).repeat(32)


def f64(x):
    return np.asarray(x).astype(np.float64)


def striped(idx):
    return np.tile(idx.reshape(-1, 16).T, (8, 1)).astype(np.uint16)


def unstriped(offs):
    return offs[:16].T.reshape(-1).astype(np.int64)


E2M1 = np.array([0.0, 0.5, 1.0, 1.5, 2.0, 3.0, 4.0, 6.0, -0.0, -0.5, -1.0, -1.5, -2.0, -3.0, -4.0, -6.0])


def pack_weight(w, fmt):
    k, n = w.shape
    w = f64(np.asarray(w, np.float32).astype(ml_dtypes.bfloat16)).reshape(k // 32, 32, n)
    amax = np.abs(w).max(1)
    if fmt == "e4m3":
        byte = np.frexp(amax)[1] - 1 + 127 - 7
    else:
        mant, ex = np.frexp(amax / 6.0)
        byte = np.where(mant > 0.5, ex, ex - 1) + 127
    byte = np.clip(np.where(amax > 0, byte, 1), 1, 254)
    scaled = (w * np.exp2(127.0 - byte)[:, None, :]).reshape(k, n).astype(np.float32)
    by_word = np.ascontiguousarray(scaled.reshape(k // 512, 128, 4, n).transpose(0, 1, 3, 2))
    if fmt == "e4m3":
        words = by_word.astype(ml_dtypes.float8_e4m3fn).view(np.uint8)
    else:
        c = by_word.astype(ml_dtypes.float4_e2m1fn).view(np.uint8) & 0xF
        words = (c[..., 0::2] | (c[..., 1::2] << 4)).reshape(k // 512, 128, 2 * n)
    return np.ascontiguousarray(words), np.ascontiguousarray(byte.astype(np.uint8).reshape(k // 512, 16, n))


def unpack_weight(words, scales, fmt):
    g, _, n = scales.shape
    words = np.ascontiguousarray(words).reshape(g, 128, n, -1)
    if fmt == "e4m3":
        vals = words.view(ml_dtypes.float8_e4m3fn).astype(np.float64)
    else:
        nib = np.empty((g, 128, n, 4), np.uint8)
        nib[..., 0::2] = words & 0xF
        nib[..., 1::2] = words >> 4
        vals = E2M1[nib]
    vals = vals * np.repeat(np.exp2(scales.astype(np.float64) - 127.0), 8, axis=1)[..., None]
    return vals.transpose(0, 1, 3, 2).reshape(g * 512, n)


def gelu(v):
    return 0.5 * v * (1.0 + np.tanh(np.sqrt(2.0 / np.pi) * (v + 0.044715 * v**3)))


def bf(x):
    return np.asarray(x, np.float32).astype(ml_dtypes.bfloat16)


def planes(Y):
    n, m = Y.shape
    b = f64(bf(Y)).reshape(n // 32, 32, m)
    amax = np.abs(b).max(1)
    byte = np.clip(np.where(amax > 0, np.frexp(amax)[1] - 1 + 127 - 7, 1), 1, 254)
    codes = (b * np.exp2(127.0 - byte)[:, None, :]).reshape(n, m).astype(np.float32).astype(ml_dtypes.float8_e4m3fn).view(np.uint8)
    words = codes.reshape(n // 512, 128, 4, m).transpose(0, 1, 3, 2)
    return np.ascontiguousarray(words), np.ascontiguousarray(byte.astype(np.uint8).reshape(n // 512, 16, m))


K, T, S, H, N, P = 1024, 4096, 1024, 512, 1024, 512

def setup_inputs():
    n = np.random.standard_normal
    s = mx_kscale(K)[:, None]
    u = mx_kscale(H)[:, None]
    tab_words, tab_scales = pack_weight(n((K, T)) * s, "e4m3")
    w2_words, w2_scales = pack_weight(1.5 * n((K, H)) * K ** -0.5 / s, "e2m1")
    w1 = 0.7 * n((K, H)) * K ** -0.5 / s * u.T
    gm = np.random.uniform(0.8, 1.6, H) * u[:, 0]
    wa = 0.67 * n((H, N)) * H ** -0.5 / u
    size = np.exp(0.8 * n(N))
    mix = 5.0 * n((N, P)) * size[:, None]
    ref = np.random.uniform(0.7, 1.4, N) * size
    return {"tab_words": tab_words, "tab_scales": tab_scales,
            "offs": striped(np.random.permutation(T)[:S]),
            "w1": w1.astype(np.float32),
            "w2_words": w2_words, "w2_scales": w2_scales,
            "gm": gm.astype(np.float32),
            "wa": wa.astype(np.float32),
            "pos1": striped(np.random.permutation(S)[:P]),
            "pos2": striped(np.random.permutation(S)[:P]),
            "mix": mix.astype(np.float32),
            "ref": ref.astype(np.float32)}

def reference(tab_words, tab_scales, offs, w1, w2_words, w2_scales, gm, wa, pos1, pos2, mix, ref):
    v = unpack_weight(tab_words, tab_scales, "e4m3")[:, unstriped(offs)]
    w2 = unpack_weight(w2_words, w2_scales, "e2m1")
    straight = mxq(f64(w1), 0, "e4m3").T @ v
    bent = np.tanh(w2.T @ v)
    h = straight + f64(gm)[:, None] * bent
    e = mxq(f64(wa), 0, "e4m3").T @ mxq(h, 0, "e4m3")
    top = e.max(axis=1)
    a = np.exp(e[:, unstriped(pos1)] - top[:, None])
    c = e[:, unstriped(pos2)]
    y = f64(mix) * a + f64(ref)[:, None] * c
    words, scales = planes(y)
    return y, words, scales

@@ -1,0 +1,301 @@
+from contextlib import ExitStack
+
+import concourse.mybir as mybir
+
+K, T, S, H, N, M = 1024, 4096, 1024, 512, 1024, 512
+FLOPS = 2 * (2 * K * H * S + H * N * S)
+
+F32 = mybir.dt.float32
+BF16 = mybir.dt.bfloat16
+I32 = mybir.dt.int32
+U32 = mybir.dt.uint32
+U16 = mybir.dt.uint16
+U8 = mybir.dt.uint8
+FP8X4 = mybir.dt.float8_e4m3fn_x4
+FP4X4 = mybir.dt.float4_e2m1fn_x4
+ACT = mybir.ActivationFunctionType
+ALU = mybir.AluOpType
+
+P = 128
+PACK = 4
+PASS = P * PACK
+HALF = 512
+AL = 64
+
+
+def tile_list_fibre_fault_desk_kernel(
+    tc, tab_words, tab_scales, offs, w1, w2_words, w2_scales, gm, wa, pos1, pos2, mix, ref,
+    out_0, out_1, out_2,
+):
+    nc = tc.nc
+    with ExitStack() as ctx:
+        keep = ctx.enter_context(tc.tile_pool(name="keep", bufs=1))
+        stage = ctx.enter_context(tc.tile_pool(name="stage", bufs=4))
+        ring = ctx.enter_context(tc.tile_pool(name="ring", bufs=3))
+        psum = ctx.enter_context(tc.psum_pool(name="psum", bufs=8))
+
+        def held(shape, dtype, name):
+            return keep.tile(shape, dtype, name=name, align_bytes=AL)
+
+        idx = keep.tile([P, S // 16], U16, name="idx")
+        p1 = keep.tile([P, M // 16], U16, name="p1")
+        p2 = keep.tile([P, M // 16], U16, name="p2")
+
+        w2_sc_raw = held([P, 2, H], U8, "w2_sc_raw")
+        nc.gpsimd.memset(w2_sc_raw[:].rearrange("p a c -> p (a c)").bitcast(I32), 0)
+        for q in range(4):
+            nc.gpsimd.dma_start(
+                out=w2_sc_raw[32 * q : 32 * q + 4, :, :].bitcast(I32),
+                in_=w2_scales[:, 4 * q : 4 * q + 4, :].rearrange("a r c -> r a c").bitcast(I32),
+            )
+
+        sc_win = held([P, T], U8, "sc_win")
+        nc.vector.memset(sc_win[32:64, :].bitcast(I32), 0)
+        nc.vector.memset(sc_win[64:128, :].bitcast(I32), 0)
+        v_sc = held([P, 2 * S], U8, "v_sc")
+        nc.vector.memset(v_sc[:].bitcast(I32), 0)
+
+        nc.sync.dma_start(idx[:], offs)
+        nc.sync.dma_start(
+            out=sc_win[0:32, :].bitcast(I32),
+            in_=tab_scales.rearrange("a q t -> q a t").bitcast(I32),
+        )
+        w2_raw = held([P, 2, 2 * H], U8, "w2_raw")
+        nc.sync.dma_start(
+            out=w2_raw[:].bitcast(I32), in_=w2_words.rearrange("a p c -> p a c").bitcast(I32)
+        )
+        tab = [held([P, T], U32, "tab%d" % a) for a in range(2)]
+        for a in range(2):
+            nc.sync.dma_start(
+                out=tab[a][:].bitcast(I32),
+                in_=tab_words[a].rearrange("p t i -> p (t i)").bitcast(I32),
+            )
+        w1_rows = w1.rearrange("(a p j) c -> a p j c", p=P, j=PACK)
+        w1_pieces = [(0, 0, H), (1, 0, H // 2), (1, H // 2, H // 2)]
+        w1_raw = []
+        for a, c0, width in w1_pieces:
+            raw = held([P, PACK, width], F32, "w1_raw%d_%d" % (a, c0))
+            nc.sync.dma_start(out=raw[:], in_=w1_rows[a, :, :, c0 : c0 + width])
+            w1_raw.append(raw)
+        gain = held([P, PACK], F32, "gain")
+        nc.sync.dma_start(out=gain[:], in_=gm.rearrange("(p t) -> p t", t=PACK))
+        wa_rows = wa.rearrange("(p j) n -> p j n", j=PACK)
+        wa_raw = [held([P, PACK, PASS], F32, "wa_raw%d" % g) for g in range(2)]
+        for g in range(2):
+            nc.sync.dma_start(out=wa_raw[g][:], in_=wa_rows[:, :, g * PASS : (g + 1) * PASS])
+        nc.sync.dma_start(p1[:], pos1)
+        nc.sync.dma_start(p2[:], pos2)
+        refs = held([P, 2, PACK], F32, "refs")
+        nc.sync.dma_start(out=refs[:], in_=ref.rearrange("(g p t) -> p g t", p=P, t=PACK))
+        mix_rows = mix.rearrange("(g p t) m -> g p t m", p=P, t=PACK)
+        mixes = [held([P, PACK, M], F32, "mix%d" % g) for g in range(2)]
+        for g in range(2):
+            nc.sync.dma_start(out=mixes[g][:], in_=mix_rows[g])
+
+        sc_picked = held([P, S], U8, "sc_picked")
+        nc.vector.tensor_copy(sc_picked[:], sc_win[:].indirect(idx[:]))
+        for q in range(4):
+            nc.gpsimd.dma_start(
+                out=v_sc[32 * q : 32 * q + 4, :].bitcast(I32),
+                in_=sc_picked[8 * q : 8 * q + 8, :].bitcast(I32),
+            )
+
+        w2_codes = held([P, 2, 2 * H], U8, "w2_codes")
+        nc.vector.tensor_copy(
+            out=w2_codes[:].rearrange("p a (t m b) -> p a m t b", t=PACK, b=2),
+            in_=w2_raw[:].rearrange("p a (m t b) -> p a m t b", t=PACK, b=2),
+        )
+        w2_sc = held([P, 2, H], U8, "w2_sc")
+        nc.vector.tensor_copy(
+            out=w2_sc[:].rearrange("p a (t m) -> p a m t", t=PACK),
+            in_=w2_sc_raw[:].rearrange("p a (m t) -> p a m t", t=PACK),
+        )
+
+        v0 = held([P, S], U32, "v0")
+        nc.vector.tensor_copy(v0[:], tab[0][:].indirect(idx[:]))
+        v1 = [held([P, HALF], U32, "v1_%d" % jh) for jh in range(2)]
+        for jh in range(2):
+            nc.vector.tensor_copy(
+                v1[jh][:], tab[1][:].indirect(idx[:, jh * HALF // 16 : (jh + 1) * HALF // 16])
+            )
+
+        def v_codes(a, jh):
+            words = v0[:, jh * HALF : (jh + 1) * HALF] if a == 0 else v1[jh][:]
+            return words.bitcast(FP8X4)
+
+        def v_scales(a, jh):
+            return v_sc[:, a * S + jh * HALF : a * S + (jh + 1) * HALF]
+
+        bent = {}
+        for jh in range(2):
+            for t in range(PACK):
+                acc = psum.tile([P, HALF], F32, name="acc")
+                for a in range(2):
+                    nc.tensor.matmul_mx(
+                        out=acc[:],
+                        lhsT=w2_codes[:, a, 2 * P * t : 2 * P * (t + 1)].bitcast(FP4X4),
+                        lhsT_scale=w2_sc[:, a, P * t : P * (t + 1)],
+                        rhs=v_codes(a, jh),
+                        rhs_scale=v_scales(a, jh),
+                        start=(a == 0),
+                        stop=(a == 1),
+                    )
+                bent[jh, t] = held([P, HALF], F32, "bent%d_%d" % (jh, t))
+                nc.scalar.activation(out=bent[jh, t][:], in_=acc[:], func=ACT.Tanh)
+
+        def quantise(grouped, name):
+            codes = held([P, PASS], U32, name + "_codes")
+            scales = held([P, PASS], U8, name + "_scales")
+            nc.vector.quantize_mx(out=codes[:].bitcast(FP8X4), scales=scales[:], in_=grouped[:])
+            return codes, scales
+
+        def deal(copy, grouped, raw, m0):
+            width = raw.shape[2] // PACK
+            copy(
+                out=grouped[:].rearrange("p (t m j) -> p m j t", t=PACK, j=PACK)[:, m0 : m0 + width],
+                in_=raw[:].rearrange("p j (m t) -> p m j t", t=PACK),
+            )
+
+        def interleave(copy, grouped, rows):
+            copy(
+                out=grouped.rearrange("p (c i t) -> p c t i", i=4, t=PACK),
+                in_=rows.rearrange("p t (c i) -> p c t i", i=4),
+            )
+
+        w1_q = []
+        for a in range(2):
+            grouped = stage.tile([P, PACK * PASS], BF16, name="grouped", align_bytes=AL)
+            for (pa, c0, width), raw in zip(w1_pieces, w1_raw):
+                if pa == a:
+                    deal(nc.vector.tensor_copy, grouped, raw, c0 // PACK)
+            w1_q.append(quantise(grouped, "w1_%d" % a))
+
+        wa_grouped = {}
+
+        def deal_wa(g):
+            wa_grouped[g] = stage.tile([P, PACK * PASS], BF16, name="grouped", align_bytes=AL)
+            deal(nc.scalar.copy, wa_grouped[g], wa_raw[g], 0)
+
+        h_grouped = {}
+
+        def make_h(jh):
+            rows = held([P, PACK, HALF], BF16, "h_rows%d" % jh)
+            for t in range(PACK):
+                acc = psum.tile([P, HALF], F32, name="acc")
+                for a in range(2):
+                    codes, scales = w1_q[a]
+                    nc.tensor.matmul_mx(
+                        out=acc[:],
+                        lhsT=codes[:, P * t : P * (t + 1)].bitcast(FP8X4),
+                        lhsT_scale=scales[:, P * t : P * (t + 1)],
+                        rhs=v_codes(a, jh),
+                        rhs_scale=v_scales(a, jh),
+                        start=(a == 0),
+                        stop=(a == 1),
+                    )
+                nc.vector.scalar_tensor_tensor(
+                    out=rows[:, t, :], in0=bent[jh, t][:], scalar=gain[:, t : t + 1], in1=acc[:],
+                    op0=ALU.mult, op1=ALU.add,
+                )
+            h_grouped[jh] = stage.tile([P, PACK * HALF], BF16, name="grouped", align_bytes=AL)
+            interleave(nc.scalar.copy, h_grouped[jh][:], rows[:])
+
+        deal_wa(0)
+        make_h(0)
+        make_h(1)
+        deal_wa(1)
+        wa_q = {0: quantise(wa_grouped[0], "wa0")}
+        h_q = {0: quantise(h_grouped[0], "h0")}
+
+        scores = [held([P, S], F32, "e%d" % i) for i in range(8)]
+        tops = held([P, 8, 2], F32, "tops")
+        neg_top = held([P, 8], F32, "neg_top")
+
+        def score(i, jh):
+            g, t = divmod(i, PACK)
+            acc = psum.tile([P, HALF], F32, name="acc")
+            nc.tensor.matmul_mx(
+                out=acc[:],
+                lhsT=wa_q[g][0][:, P * t : P * (t + 1)].bitcast(FP8X4),
+                lhsT_scale=wa_q[g][1][:, P * t : P * (t + 1)],
+                rhs=h_q[jh][0][:].bitcast(FP8X4),
+                rhs_scale=h_q[jh][1][:],
+                start=True,
+                stop=True,
+            )
+            nc.vector.tensor_scalar(
+                out=scores[i][:, jh * HALF : (jh + 1) * HALF], in0=acc[:], scalar1=1.0, scalar2=None,
+                op0=ALU.mult, op1=ALU.max, accum_out=tops[:, i, jh : jh + 1],
+            )
+
+        y = [held([P, PACK, M], F32, "y%d" % g) for g in range(2)]
+        y_rows = out_0.rearrange("(g p t) m -> g p t m", p=P, t=PACK)
+        y_scales = held([P, 2, M], U8, "y_scales")
+        looked, picked = {}, {}
+
+        def look(i):
+            nc.gpsimd.tensor_scalar(
+                out=neg_top[:, i : i + 1], in0=tops[:, i, 0:1], scalar1=tops[:, i, 1:2], scalar2=-1.0,
+                op0=ALU.max, op1=ALU.mult,
+            )
+            looked[i] = ring.tile([P, M], F32, name="looked")
+            nc.scalar.activation(
+                out=looked[i][:], in_=scores[i][:].indirect(p1[:]), func=ACT.Exp,
+                bias=neg_top[:, i : i + 1],
+            )
+
+        def pick(i):
+            picked[i] = ring.tile([P, M], F32, name="picked")
+            nc.vector.tensor_copy(picked[i][:], scores[i][:].indirect(p2[:]))
+
+        def finish(i):
+            g, t = divmod(i, PACK)
+            mixed = ring.tile([P, M], F32, name="mixed")
+            nc.vector.tensor_tensor(out=mixed[:], in0=looked[i][:], in1=mixes[g][:, t, :], op=ALU.mult)
+            nc.vector.scalar_tensor_tensor(
+                out=y[g][:, t, :], in0=picked[i][:], scalar=refs[:, g, t : t + 1], in1=mixed[:],
+                op0=ALU.mult, op1=ALU.add,
+            )
+            nc.sync.dma_start(out=y_rows[g, :, t, :], in_=y[g][:, t, :])
+
+        y_grouped = {}
+
+        def group_y(g, copy):
+            y_grouped[g] = stage.tile([P, PACK * M], BF16, name="grouped", align_bytes=AL)
+            interleave(copy, y_grouped[g][:], y[g][:])
+
+        def planes(g):
+            codes = held([P, M], U32, "y_codes%d" % g)
+            nc.vector.quantize_mx(
+                out=codes[:].bitcast(FP8X4), scales=y_scales[:, g, :], in_=y_grouped[g][:]
+            )
+            nc.sync.dma_start(
+                out=out_1[g].rearrange("p m t -> p (m t)").bitcast(I32), in_=codes[:].bitcast(I32)
+            )
+
+        for i in range(PACK):
+            score(i, 0)
+        h_q[1] = quantise(h_grouped[1], "h1")
+        for i in range(8):
+            if i == 2:
+                wa_q[1] = quantise(wa_grouped[1], "wa1")
+            if i >= PACK:
+                score(i, 0)
+            score(i, 1)
+            look(i)
+            if i >= 1:
+                finish(i - 1)
+            if i == PACK:
+                group_y(0, nc.scalar.copy)
+            pick(i)
+            if i == PACK + 2:
+                planes(0)
+        finish(7)
+        group_y(1, nc.vector.tensor_copy)
+        planes(1)
+        for q in range(4):
+            eng = nc.scalar if q % 2 else nc.sync
+            eng.dma_start(
+                out=out_2[:, 4 * q : 4 * q + 4, :].rearrange("g r m -> r g m").bitcast(I32),
+                in_=y_scales[32 * q : 32 * q + 4, :, :].bitcast(I32),
+            )

@@ -43,15 +43,9 @@ def tile_list_fibre_fault_desk_kernel(
 
         w2_sc_raw = held([P, 2, H], U8, "w2_sc_raw")
         nc.gpsimd.memset(w2_sc_raw[:].rearrange("p a c -> p (a c)").bitcast(I32), 0)
-        for q in range(4):
-            nc.gpsimd.dma_start(
-                out=w2_sc_raw[32 * q : 32 * q + 4, :, :].bitcast(I32),
-                in_=w2_scales[:, 4 * q : 4 * q + 4, :].rearrange("a r c -> r a c").bitcast(I32),
-            )
-
-        sc_win = held([P, T], U8, "sc_win")
+        sc_win = keep.tile([P, T], U8, name="sc_win", tag="reused", align_bytes=AL)
         nc.vector.memset(sc_win[32:64, :].bitcast(I32), 0)
-        nc.vector.memset(sc_win[64:128, :].bitcast(I32), 0)
+        nc.gpsimd.memset(sc_win[64:128, :].bitcast(I32), 0)
         v_sc = held([P, 2 * S], U8, "v_sc")
         nc.vector.memset(v_sc[:].bitcast(I32), 0)
 
@@ -64,41 +58,53 @@ def tile_list_fibre_fault_desk_kernel(
         nc.sync.dma_start(
             out=w2_raw[:].bitcast(I32), in_=w2_words.rearrange("a p c -> p a c").bitcast(I32)
         )
+        for q in range(4):
+            nc.sync.dma_start(
+                out=w2_sc_raw[32 * q : 32 * q + 4, :, :].bitcast(I32),
+                in_=w2_scales[:, 4 * q : 4 * q + 4, :].rearrange("a r c -> r a c").bitcast(I32),
+            )
         tab = [held([P, T], U32, "tab%d" % a) for a in range(2)]
         for a in range(2):
             nc.sync.dma_start(
                 out=tab[a][:].bitcast(I32),
                 in_=tab_words[a].rearrange("p t i -> p (t i)").bitcast(I32),
             )
-        w1_rows = w1.rearrange("(a p j) c -> a p j c", p=P, j=PACK)
-        w1_pieces = [(0, 0, H), (1, 0, H // 2), (1, H // 2, H // 2)]
-        w1_raw = []
-        for a, c0, width in w1_pieces:
-            raw = held([P, PACK, width], F32, "w1_raw%d_%d" % (a, c0))
-            nc.sync.dma_start(out=raw[:], in_=w1_rows[a, :, :, c0 : c0 + width])
-            w1_raw.append(raw)
-        gain = held([P, PACK], F32, "gain")
-        nc.sync.dma_start(out=gain[:], in_=gm.rearrange("(p t) -> p t", t=PACK))
-        wa_rows = wa.rearrange("(p j) n -> p j n", j=PACK)
-        wa_raw = [held([P, PACK, PASS], F32, "wa_raw%d" % g) for g in range(2)]
-        for g in range(2):
-            nc.sync.dma_start(out=wa_raw[g][:], in_=wa_rows[:, :, g * PASS : (g + 1) * PASS])
         nc.sync.dma_start(p1[:], pos1)
         nc.sync.dma_start(p2[:], pos2)
-        refs = held([P, 2, PACK], F32, "refs")
-        nc.sync.dma_start(out=refs[:], in_=ref.rearrange("(g p t) -> p g t", p=P, t=PACK))
-        mix_rows = mix.rearrange("(g p t) m -> g p t m", p=P, t=PACK)
-        mixes = [held([P, PACK, M], F32, "mix%d" % g) for g in range(2)]
-        for g in range(2):
-            nc.sync.dma_start(out=mixes[g][:], in_=mix_rows[g])
 
         sc_picked = held([P, S], U8, "sc_picked")
         nc.vector.tensor_copy(sc_picked[:], sc_win[:].indirect(idx[:]))
         for q in range(4):
-            nc.gpsimd.dma_start(
+            nc.sync.dma_start(
                 out=v_sc[32 * q : 32 * q + 4, :].bitcast(I32),
                 in_=sc_picked[8 * q : 8 * q + 8, :].bitcast(I32),
             )
+
+        block = PACK * PASS
+        floats = keep.tile([P, 6 * block + 16], F32, name="floats", tag="reused", align_bytes=AL)
+
+        def rows4(c0, width):
+            return floats[:, c0 : c0 + PACK * width].rearrange("p (j c) -> p j c", j=PACK)
+
+        w1_rows = w1.rearrange("(a p j) c -> a p j c", p=P, j=PACK)
+        w1_pieces = [(0, 0, H), (1, 0, H // 2), (1, H // 2, H // 2)]
+        w1_raw = []
+        for a, c0, width in w1_pieces:
+            raw = rows4(a * block + PACK * c0, width)
+            nc.sync.dma_start(out=raw, in_=w1_rows[a, :, :, c0 : c0 + width])
+            w1_raw.append(raw)
+        gain = floats[:, 6 * block : 6 * block + PACK]
+        nc.sync.dma_start(out=gain, in_=gm.rearrange("(p t) -> p t", t=PACK))
+        wa_rows = wa.rearrange("(p j) n -> p j n", j=PACK)
+        wa_raw = [rows4((2 + g) * block, PASS) for g in range(2)]
+        for g in range(2):
+            nc.sync.dma_start(out=wa_raw[g], in_=wa_rows[:, :, g * PASS : (g + 1) * PASS])
+        refs = floats[:, 6 * block + 8 : 6 * block + 16].rearrange("p (g t) -> p g t", g=2)
+        nc.sync.dma_start(out=refs, in_=ref.rearrange("(g p t) -> p g t", p=P, t=PACK))
+        mix_rows = mix.rearrange("(g p t) m -> g p t m", p=P, t=PACK)
+        mixes = [rows4((4 + g) * block, M) for g in range(2)]
+        for g in range(2):
+            nc.sync.dma_start(out=mixes[g], in_=mix_rows[g])
 
         w2_codes = held([P, 2, 2 * H], U8, "w2_codes")
         nc.vector.tensor_copy(
@@ -153,7 +159,7 @@ def tile_list_fibre_fault_desk_kernel(
             width = raw.shape[2] // PACK
             copy(
                 out=grouped[:].rearrange("p (t m j) -> p m j t", t=PACK, j=PACK)[:, m0 : m0 + width],
-                in_=raw[:].rearrange("p j (m t) -> p m j t", t=PACK),
+                in_=raw.rearrange("p j (m t) -> p m j t", t=PACK),
             )
 
         def interleave(copy, grouped, rows):
@@ -172,9 +178,11 @@ def tile_list_fibre_fault_desk_kernel(
 
         wa_grouped = {}
 
-        def deal_wa(g):
+        def deal_wa(g, pieces):
             wa_grouped[g] = stage.tile([P, PACK * PASS], BF16, name="grouped", align_bytes=AL)
-            deal(nc.scalar.copy, wa_grouped[g], wa_raw[g], 0)
+            width = PASS // pieces
+            for c0 in range(0, PASS, width):
+                deal(nc.scalar.copy, wa_grouped[g], wa_raw[g][:, :, c0 : c0 + width], c0 // PACK)
 
         h_grouped = {}
 
@@ -200,16 +208,15 @@ def tile_list_fibre_fault_desk_kernel(
             h_grouped[jh] = stage.tile([P, PACK * HALF], BF16, name="grouped", align_bytes=AL)
             interleave(nc.scalar.copy, h_grouped[jh][:], rows[:])
 
-        deal_wa(0)
+        deal_wa(0, 1)
         make_h(0)
         make_h(1)
-        deal_wa(1)
         wa_q = {0: quantise(wa_grouped[0], "wa0")}
         h_q = {0: quantise(h_grouped[0], "h0")}
 
         scores = [held([P, S], F32, "e%d" % i) for i in range(8)]
-        tops = held([P, 8, 2], F32, "tops")
         neg_top = held([P, 8], F32, "neg_top")
+        tops = {}
 
         def score(i, jh):
             g, t = divmod(i, PACK)
@@ -223,9 +230,12 @@ def tile_list_fibre_fault_desk_kernel(
                 start=True,
                 stop=True,
             )
+            tag = "mixed%d" % (i % 2) if jh else "picked%d" % (i % 4)
+            tops[i, jh] = keep.tile([P, 1], F32, name="top", tag=tag)
             nc.vector.tensor_scalar(
-                out=scores[i][:, jh * HALF : (jh + 1) * HALF], in0=acc[:], scalar1=1.0, scalar2=None,
-                op0=ALU.mult, op1=ALU.max, accum_out=tops[:, i, jh : jh + 1],
+                out=scores[i][:, jh * HALF : (jh + 1) * HALF], in0=acc[:], scalar1=1.0,
+                scalar2=tops[i, 0][:] if jh else None,
+                op0=ALU.mult, op1=ALU.max, accum_out=tops[i, jh][:],
             )
 
         y = [held([P, PACK, M], F32, "y%d" % g) for g in range(2)]
@@ -234,9 +244,8 @@ def tile_list_fibre_fault_desk_kernel(
         looked, picked = {}, {}
 
         def look(i):
-            nc.gpsimd.tensor_scalar(
-                out=neg_top[:, i : i + 1], in0=tops[:, i, 0:1], scalar1=tops[:, i, 1:2], scalar2=-1.0,
-                op0=ALU.max, op1=ALU.mult,
+            nc.scalar.activation(
+                out=neg_top[:, i : i + 1], in_=tops[i, 1][:], func=ACT.Copy, scale=-1.0
             )
             looked[i] = ring.tile([P, M], F32, name="looked")
             nc.scalar.activation(
@@ -245,13 +254,14 @@ def tile_list_fibre_fault_desk_kernel(
             )
 
         def pick(i):
-            picked[i] = ring.tile([P, M], F32, name="picked")
+            picked[i] = keep.tile([P, M], F32, name="picked", tag="picked%d" % (i % 4))
             nc.vector.tensor_copy(picked[i][:], scores[i][:].indirect(p2[:]))
 
         def finish(i):
             g, t = divmod(i, PACK)
-            mixed = ring.tile([P, M], F32, name="mixed")
-            nc.vector.tensor_tensor(out=mixed[:], in0=looked[i][:], in1=mixes[g][:, t, :], op=ALU.mult)
+            mixed = keep.tile([P, M], F32, name="mixed", tag="mixed%d" % (i % 2))
+            eng = nc.vector if i == 7 else nc.gpsimd
+            eng.tensor_tensor(out=mixed[:], in0=looked[i][:], in1=mixes[g][:, t, :], op=ALU.mult)
             nc.vector.scalar_tensor_tensor(
                 out=y[g][:, t, :], in0=picked[i][:], scalar=refs[:, g, t : t + 1], in1=mixed[:],
                 op0=ALU.mult, op1=ALU.add,
@@ -260,9 +270,10 @@ def tile_list_fibre_fault_desk_kernel(
 
         y_grouped = {}
 
-        def group_y(g, copy):
+        def group_y(g, shares):
             y_grouped[g] = stage.tile([P, PACK * M], BF16, name="grouped", align_bytes=AL)
-            interleave(copy, y_grouped[g][:], y[g][:])
+            for copy, m0, m1 in shares:
+                interleave(copy, y_grouped[g][:, PACK * m0 : PACK * m1], y[g][:, :, m0:m1])
 
         def planes(g):
             codes = held([P, M], U32, "y_codes%d" % g)
@@ -273,25 +284,27 @@ def tile_list_fibre_fault_desk_kernel(
                 out=out_1[g].rearrange("p m t -> p (m t)").bitcast(I32), in_=codes[:].bitcast(I32)
             )
 
-        for i in range(PACK):
-            score(i, 0)
+        score(0, 0)
+        score(1, 0)
         h_q[1] = quantise(h_grouped[1], "h1")
         for i in range(8):
             if i == 2:
                 wa_q[1] = quantise(wa_grouped[1], "wa1")
-            if i >= PACK:
-                score(i, 0)
+            if i + 2 < 8:
+                score(i + 2, 0)
             score(i, 1)
             look(i)
+            if i == 0:
+                deal_wa(1, 4)
+            pick(i)
             if i >= 1:
                 finish(i - 1)
-            if i == PACK:
-                group_y(0, nc.scalar.copy)
-            pick(i)
-            if i == PACK + 2:
+            if i == PACK + 1:
+                group_y(0, [(nc.scalar.copy, m0, m0 + 128) for m0 in range(0, M, 128)])
+            if i == 6:
                 planes(0)
         finish(7)
-        group_y(1, nc.vector.tensor_copy)
+        group_y(1, [(nc.vector.tensor_copy, 0, 352), (nc.scalar.copy, 352, M)])
         planes(1)
         for q in range(4):
             eng = nc.scalar if q % 2 else nc.sync

@@ -149,10 +149,16 @@ def tile_list_fibre_fault_desk_kernel(
                 bent[jh, t] = held([P, HALF], F32, "bent%d_%d" % (jh, t))
                 nc.scalar.activation(out=bent[jh, t][:], in_=acc[:], func=ACT.Tanh)
 
-        def quantise(grouped, name):
+        def quantise(grouped, name, pieces=1):
             codes = held([P, PASS], U32, name + "_codes")
             scales = held([P, PASS], U8, name + "_scales")
-            nc.vector.quantize_mx(out=codes[:].bitcast(FP8X4), scales=scales[:], in_=grouped[:])
+            width = PASS // pieces
+            for c0 in range(0, PASS, width):
+                nc.vector.quantize_mx(
+                    out=codes[:, c0 : c0 + width].bitcast(FP8X4),
+                    scales=scales[:, c0 : c0 + width],
+                    in_=grouped[:, PACK * c0 : PACK * (c0 + width)],
+                )
             return codes, scales
 
         def deal(copy, grouped, raw, m0):
@@ -174,7 +180,7 @@ def tile_list_fibre_fault_desk_kernel(
             for (pa, c0, width), raw in zip(w1_pieces, w1_raw):
                 if pa == a:
                     deal(nc.vector.tensor_copy, grouped, raw, c0 // PACK)
-            w1_q.append(quantise(grouped, "w1_%d" % a))
+            w1_q.append(quantise(grouped, "w1_%d" % a, PACK if a else 1))
 
         wa_grouped = {}
 
@@ -210,13 +216,14 @@ def tile_list_fibre_fault_desk_kernel(
 
         deal_wa(0, 1)
         make_h(0)
-        make_h(1)
         wa_q = {0: quantise(wa_grouped[0], "wa0")}
         h_q = {0: quantise(h_grouped[0], "h0")}
+        make_h(1)
+        deal_wa(1, 4)
 
         scores = [held([P, S], F32, "e%d" % i) for i in range(8)]
         neg_top = held([P, 8], F32, "neg_top")
-        tops = {}
+        tops = held([P, 2, 8], F32, "tops")
 
         def score(i, jh):
             g, t = divmod(i, PACK)
@@ -230,12 +237,10 @@ def tile_list_fibre_fault_desk_kernel(
                 start=True,
                 stop=True,
             )
-            tag = "mixed%d" % (i % 2) if jh else "picked%d" % (i % 4)
-            tops[i, jh] = keep.tile([P, 1], F32, name="top", tag=tag)
             nc.vector.tensor_scalar(
                 out=scores[i][:, jh * HALF : (jh + 1) * HALF], in0=acc[:], scalar1=1.0,
-                scalar2=tops[i, 0][:] if jh else None,
-                op0=ALU.mult, op1=ALU.max, accum_out=tops[i, jh][:],
+                scalar2=tops[:, 0, i : i + 1] if jh else None,
+                op0=ALU.mult, op1=ALU.max, accum_out=tops[:, jh, i : i + 1],
             )
 
         y = [held([P, PACK, M], F32, "y%d" % g) for g in range(2)]
@@ -245,7 +250,7 @@ def tile_list_fibre_fault_desk_kernel(
 
         def look(i):
             nc.scalar.activation(
-                out=neg_top[:, i : i + 1], in_=tops[i, 1][:], func=ACT.Copy, scale=-1.0
+                out=neg_top[:, i : i + 1], in_=tops[:, 1, i : i + 1], func=ACT.Copy, scale=-1.0
             )
             looked[i] = ring.tile([P, M], F32, name="looked")
             nc.scalar.activation(
@@ -254,18 +259,25 @@ def tile_list_fibre_fault_desk_kernel(
             )
 
         def pick(i):
-            picked[i] = keep.tile([P, M], F32, name="picked", tag="picked%d" % (i % 4))
+            picked[i] = ring.tile([P, M], F32, name="picked")
             nc.vector.tensor_copy(picked[i][:], scores[i][:].indirect(p2[:]))
 
         def finish(i):
             g, t = divmod(i, PACK)
-            mixed = keep.tile([P, M], F32, name="mixed", tag="mixed%d" % (i % 2))
+            mixed = ring.tile([P, M], F32, name="mixed")
             eng = nc.vector if i == 7 else nc.gpsimd
             eng.tensor_tensor(out=mixed[:], in0=looked[i][:], in1=mixes[g][:, t, :], op=ALU.mult)
-            nc.vector.scalar_tensor_tensor(
-                out=y[g][:, t, :], in0=picked[i][:], scalar=refs[:, g, t : t + 1], in1=mixed[:],
-                op0=ALU.mult, op1=ALU.add,
-            )
+            if i < 6:
+                scaled = ring.tile([P, M], F32, name="scaled")
+                nc.scalar.activation(
+                    out=scaled[:], in_=picked[i][:], func=ACT.Copy, scale=refs[:, g, t : t + 1]
+                )
+                nc.gpsimd.tensor_tensor(out=y[g][:, t, :], in0=scaled[:], in1=mixed[:], op=ALU.add)
+            else:
+                nc.vector.scalar_tensor_tensor(
+                    out=y[g][:, t, :], in0=picked[i][:], scalar=refs[:, g, t : t + 1], in1=mixed[:],
+                    op0=ALU.mult, op1=ALU.add,
+                )
             nc.sync.dma_start(out=y_rows[g, :, t, :], in_=y[g][:, t, :])
 
         y_grouped = {}
@@ -288,18 +300,18 @@ def tile_list_fibre_fault_desk_kernel(
         score(1, 0)
         h_q[1] = quantise(h_grouped[1], "h1")
         for i in range(8):
-            if i == 2:
-                wa_q[1] = quantise(wa_grouped[1], "wa1")
-            if i + 2 < 8:
-                score(i + 2, 0)
             score(i, 1)
             look(i)
             if i == 0:
-                deal_wa(1, 4)
+                wa_q[1] = quantise(wa_grouped[1], "wa1")
+            if i + 2 < 8:
+                score(i + 2, 0)
+            if i == 7:
+                finish(6)
             pick(i)
-            if i >= 1:
-                finish(i - 1)
-            if i == PACK + 1:
+            if i < 6:
+                finish(i)
+            if i == PACK:
                 group_y(0, [(nc.scalar.copy, m0, m0 + 128) for m0 in range(0, M, 128)])
             if i == 6:
                 planes(0)

@@ -21,6 +21,8 @@ PACK = 4
 PASS = P * PACK
 HALF = 512
 AL = 64
+AHEAD = 2
+ON_VECTOR = (5, 6, 7)
 
 
 def tile_list_fibre_fault_desk_kernel(
@@ -31,7 +33,7 @@ def tile_list_fibre_fault_desk_kernel(
     with ExitStack() as ctx:
         keep = ctx.enter_context(tc.tile_pool(name="keep", bufs=1))
         stage = ctx.enter_context(tc.tile_pool(name="stage", bufs=4))
-        ring = ctx.enter_context(tc.tile_pool(name="ring", bufs=3))
+        ring = ctx.enter_context(tc.tile_pool(name="ring", bufs=4))
         psum = ctx.enter_context(tc.psum_pool(name="psum", bufs=8))
 
         def held(shape, dtype, name):
@@ -212,11 +214,14 @@ def tile_list_fibre_fault_desk_kernel(
                     op0=ALU.mult, op1=ALU.add,
                 )
             h_grouped[jh] = stage.tile([P, PACK * HALF], BF16, name="grouped", align_bytes=AL)
-            interleave(nc.scalar.copy, h_grouped[jh][:], rows[:])
+            split = HALF // 2 if jh else HALF
+            interleave(nc.scalar.copy, h_grouped[jh][:, : PACK * split], rows[:, :, :split])
+            if jh:
+                interleave(nc.vector.tensor_copy, h_grouped[jh][:, PACK * split :], rows[:, :, split:])
 
         deal_wa(0, 1)
-        make_h(0)
         wa_q = {0: quantise(wa_grouped[0], "wa0")}
+        make_h(0)
         h_q = {0: quantise(h_grouped[0], "h0")}
         make_h(1)
         deal_wa(1, 4)
@@ -246,16 +251,21 @@ def tile_list_fibre_fault_desk_kernel(
         y = [held([P, PACK, M], F32, "y%d" % g) for g in range(2)]
         y_rows = out_0.rearrange("(g p t) m -> g p t m", p=P, t=PACK)
         y_scales = held([P, 2, M], U8, "y_scales")
-        looked, picked = {}, {}
+        looked, picked, mixed = {}, {}, {}
 
         def look(i):
             nc.scalar.activation(
                 out=neg_top[:, i : i + 1], in_=tops[:, 1, i : i + 1], func=ACT.Copy, scale=-1.0
             )
+            g, t = divmod(i, PACK)
             looked[i] = ring.tile([P, M], F32, name="looked")
             nc.scalar.activation(
                 out=looked[i][:], in_=scores[i][:].indirect(p1[:]), func=ACT.Exp,
                 bias=neg_top[:, i : i + 1],
+            )
+            mixed[i] = ring.tile([P, M], F32, name="mixed")
+            nc.gpsimd.tensor_tensor(
+                out=mixed[i][:], in0=looked[i][:], in1=mixes[g][:, t, :], op=ALU.mult
             )
 
         def pick(i):
@@ -264,18 +274,15 @@ def tile_list_fibre_fault_desk_kernel(
 
         def finish(i):
             g, t = divmod(i, PACK)
-            mixed = ring.tile([P, M], F32, name="mixed")
-            eng = nc.vector if i == 7 else nc.gpsimd
-            eng.tensor_tensor(out=mixed[:], in0=looked[i][:], in1=mixes[g][:, t, :], op=ALU.mult)
-            if i < 6:
+            if i not in ON_VECTOR:
                 scaled = ring.tile([P, M], F32, name="scaled")
                 nc.scalar.activation(
                     out=scaled[:], in_=picked[i][:], func=ACT.Copy, scale=refs[:, g, t : t + 1]
                 )
-                nc.gpsimd.tensor_tensor(out=y[g][:, t, :], in0=scaled[:], in1=mixed[:], op=ALU.add)
+                nc.gpsimd.tensor_tensor(out=y[g][:, t, :], in0=scaled[:], in1=mixed[i][:], op=ALU.add)
             else:
                 nc.vector.scalar_tensor_tensor(
-                    out=y[g][:, t, :], in0=picked[i][:], scalar=refs[:, g, t : t + 1], in1=mixed[:],
+                    out=y[g][:, t, :], in0=picked[i][:], scalar=refs[:, g, t : t + 1], in1=mixed[i][:],
                     op0=ALU.mult, op1=ALU.add,
                 )
             nc.sync.dma_start(out=y_rows[g, :, t, :], in_=y[g][:, t, :])
@@ -296,26 +303,29 @@ def tile_list_fibre_fault_desk_kernel(
                 out=out_1[g].rearrange("p m t -> p (m t)").bitcast(I32), in_=codes[:].bitcast(I32)
             )
 
-        score(0, 0)
-        score(1, 0)
         h_q[1] = quantise(h_grouped[1], "h1")
-        for i in range(8):
-            score(i, 1)
-            look(i)
-            if i == 0:
+        score(0, 0)
+        for step in range(8 + AHEAD):
+            if step < 8:
+                score(step, 1)
+                look(step)
+            if step == 0:
+                score(1, 0)
+            if step == 1:
                 wa_q[1] = quantise(wa_grouped[1], "wa1")
-            if i + 2 < 8:
-                score(i + 2, 0)
+            if step + 2 < 8:
+                score(step + 2, 0)
+            i = step - AHEAD
+            if i >= 0:
+                pick(i)
+                if i not in ON_VECTOR:
+                    finish(i)
+            if step == 7:
+                group_y(0, [(nc.scalar.copy, 0, M)])
+        for i in ON_VECTOR:
             if i == 7:
-                finish(6)
-            pick(i)
-            if i < 6:
-                finish(i)
-            if i == PACK:
-                group_y(0, [(nc.scalar.copy, m0, m0 + 128) for m0 in range(0, M, 128)])
-            if i == 6:
                 planes(0)
-        finish(7)
+            finish(i)
         group_y(1, [(nc.vector.tensor_copy, 0, 352), (nc.scalar.copy, 352, M)])
         planes(1)
         for q in range(4):

from contextlib import ExitStack

import concourse.mybir as mybir

K, T, S, H, N, M = 1024, 4096, 1024, 512, 1024, 512
FLOPS = 2 * (2 * K * H * S + H * N * S)

F32 = mybir.dt.float32
BF16 = mybir.dt.bfloat16
I32 = mybir.dt.int32
U32 = mybir.dt.uint32
U16 = mybir.dt.uint16
U8 = mybir.dt.uint8
FP8X4 = mybir.dt.float8_e4m3fn_x4
FP4X4 = mybir.dt.float4_e2m1fn_x4
ACT = mybir.ActivationFunctionType
ALU = mybir.AluOpType

P = 128
PACK = 4
PASS = P * PACK
HALF = 512
AL = 64
AHEAD = 2
ON_VECTOR = (5, 6, 7)


def tile_list_fibre_fault_desk_kernel(
    tc, tab_words, tab_scales, offs, w1, w2_words, w2_scales, gm, wa, pos1, pos2, mix, ref,
    out_0, out_1, out_2,
):
    nc = tc.nc
    with ExitStack() as ctx:
        keep = ctx.enter_context(tc.tile_pool(name="keep", bufs=1))
        stage = ctx.enter_context(tc.tile_pool(name="stage", bufs=4))
        ring = ctx.enter_context(tc.tile_pool(name="ring", bufs=4))
        psum = ctx.enter_context(tc.psum_pool(name="psum", bufs=8))

        def held(shape, dtype, name):
            return keep.tile(shape, dtype, name=name, align_bytes=AL)

        idx = keep.tile([P, S // 16], U16, name="idx")
        p1 = keep.tile([P, M // 16], U16, name="p1")
        p2 = keep.tile([P, M // 16], U16, name="p2")

        w2_sc_raw = held([P, 2, H], U8, "w2_sc_raw")
        nc.gpsimd.memset(w2_sc_raw[:].rearrange("p a c -> p (a c)").bitcast(I32), 0)
        sc_win = keep.tile([P, T], U8, name="sc_win", tag="reused", align_bytes=AL)
        nc.vector.memset(sc_win[32:64, :].bitcast(I32), 0)
        nc.gpsimd.memset(sc_win[64:128, :].bitcast(I32), 0)
        v_sc = held([P, 2 * S], U8, "v_sc")
        nc.vector.memset(v_sc[:].bitcast(I32), 0)

        nc.sync.dma_start(idx[:], offs)
        nc.sync.dma_start(
            out=sc_win[0:32, :].bitcast(I32),
            in_=tab_scales.rearrange("a q t -> q a t").bitcast(I32),
        )
        w2_raw = held([P, 2, 2 * H], U8, "w2_raw")
        nc.sync.dma_start(
            out=w2_raw[:].bitcast(I32), in_=w2_words.rearrange("a p c -> p a c").bitcast(I32)
        )
        for q in range(4):
            nc.sync.dma_start(
                out=w2_sc_raw[32 * q : 32 * q + 4, :, :].bitcast(I32),
                in_=w2_scales[:, 4 * q : 4 * q + 4, :].rearrange("a r c -> r a c").bitcast(I32),
            )
        tab = [held([P, T], U32, "tab%d" % a) for a in range(2)]
        for a in range(2):
            nc.sync.dma_start(
                out=tab[a][:].bitcast(I32),
                in_=tab_words[a].rearrange("p t i -> p (t i)").bitcast(I32),
            )
        nc.sync.dma_start(p1[:], pos1)
        nc.sync.dma_start(p2[:], pos2)

        sc_picked = held([P, S], U8, "sc_picked")
        nc.vector.tensor_copy(sc_picked[:], sc_win[:].indirect(idx[:]))
        for q in range(4):
            nc.sync.dma_start(
                out=v_sc[32 * q : 32 * q + 4, :].bitcast(I32),
                in_=sc_picked[8 * q : 8 * q + 8, :].bitcast(I32),
            )

        block = PACK * PASS
        floats = keep.tile([P, 6 * block + 16], F32, name="floats", tag="reused", align_bytes=AL)

        def rows4(c0, width):
            return floats[:, c0 : c0 + PACK * width].rearrange("p (j c) -> p j c", j=PACK)

        w1_rows = w1.rearrange("(a p j) c -> a p j c", p=P, j=PACK)
        w1_pieces = [(0, 0, H), (1, 0, H // 2), (1, H // 2, H // 2)]
        w1_raw = []
        for a, c0, width in w1_pieces:
            raw = rows4(a * block + PACK * c0, width)
            nc.sync.dma_start(out=raw, in_=w1_rows[a, :, :, c0 : c0 + width])
            w1_raw.append(raw)
        gain = floats[:, 6 * block : 6 * block + PACK]
        nc.sync.dma_start(out=gain, in_=gm.rearrange("(p t) -> p t", t=PACK))
        wa_rows = wa.rearrange("(p j) n -> p j n", j=PACK)
        wa_raw = [rows4((2 + g) * block, PASS) for g in range(2)]
        for g in range(2):
            nc.sync.dma_start(out=wa_raw[g], in_=wa_rows[:, :, g * PASS : (g + 1) * PASS])
        refs = floats[:, 6 * block + 8 : 6 * block + 16].rearrange("p (g t) -> p g t", g=2)
        nc.sync.dma_start(out=refs, in_=ref.rearrange("(g p t) -> p g t", p=P, t=PACK))
        mix_rows = mix.rearrange("(g p t) m -> g p t m", p=P, t=PACK)
        mixes = [rows4((4 + g) * block, M) for g in range(2)]
        for g in range(2):
            nc.sync.dma_start(out=mixes[g], in_=mix_rows[g])

        w2_codes = held([P, 2, 2 * H], U8, "w2_codes")
        nc.vector.tensor_copy(
            out=w2_codes[:].rearrange("p a (t m b) -> p a m t b", t=PACK, b=2),
            in_=w2_raw[:].rearrange("p a (m t b) -> p a m t b", t=PACK, b=2),
        )
        w2_sc = held([P, 2, H], U8, "w2_sc")
        nc.vector.tensor_copy(
            out=w2_sc[:].rearrange("p a (t m) -> p a m t", t=PACK),
            in_=w2_sc_raw[:].rearrange("p a (m t) -> p a m t", t=PACK),
        )

        v0 = held([P, S], U32, "v0")
        nc.vector.tensor_copy(v0[:], tab[0][:].indirect(idx[:]))
        v1 = [held([P, HALF], U32, "v1_%d" % jh) for jh in range(2)]
        for jh in range(2):
            nc.vector.tensor_copy(
                v1[jh][:], tab[1][:].indirect(idx[:, jh * HALF // 16 : (jh + 1) * HALF // 16])
            )

        def v_codes(a, jh):
            words = v0[:, jh * HALF : (jh + 1) * HALF] if a == 0 else v1[jh][:]
            return words.bitcast(FP8X4)

        def v_scales(a, jh):
            return v_sc[:, a * S + jh * HALF : a * S + (jh + 1) * HALF]

        bent = {}
        for jh in range(2):
            for t in range(PACK):
                acc = psum.tile([P, HALF], F32, name="acc")
                for a in range(2):
                    nc.tensor.matmul_mx(
                        out=acc[:],
                        lhsT=w2_codes[:, a, 2 * P * t : 2 * P * (t + 1)].bitcast(FP4X4),
                        lhsT_scale=w2_sc[:, a, P * t : P * (t + 1)],
                        rhs=v_codes(a, jh),
                        rhs_scale=v_scales(a, jh),
                        start=(a == 0),
                        stop=(a == 1),
                    )
                bent[jh, t] = held([P, HALF], F32, "bent%d_%d" % (jh, t))
                nc.scalar.activation(out=bent[jh, t][:], in_=acc[:], func=ACT.Tanh)

        def quantise(grouped, name, pieces=1):
            codes = held([P, PASS], U32, name + "_codes")
            scales = held([P, PASS], U8, name + "_scales")
            width = PASS // pieces
            for c0 in range(0, PASS, width):
                nc.vector.quantize_mx(
                    out=codes[:, c0 : c0 + width].bitcast(FP8X4),
                    scales=scales[:, c0 : c0 + width],
                    in_=grouped[:, PACK * c0 : PACK * (c0 + width)],
                )
            return codes, scales

        def deal(copy, grouped, raw, m0):
            width = raw.shape[2] // PACK
            copy(
                out=grouped[:].rearrange("p (t m j) -> p m j t", t=PACK, j=PACK)[:, m0 : m0 + width],
                in_=raw.rearrange("p j (m t) -> p m j t", t=PACK),
            )

        def interleave(copy, grouped, rows):
            copy(
                out=grouped.rearrange("p (c i t) -> p c t i", i=4, t=PACK),
                in_=rows.rearrange("p t (c i) -> p c t i", i=4),
            )

        w1_q = []
        for a in range(2):
            grouped = stage.tile([P, PACK * PASS], BF16, name="grouped", align_bytes=AL)
            for (pa, c0, width), raw in zip(w1_pieces, w1_raw):
                if pa == a:
                    deal(nc.vector.tensor_copy, grouped, raw, c0 // PACK)
            w1_q.append(quantise(grouped, "w1_%d" % a, PACK if a else 1))

        wa_grouped = {}

        def deal_wa(g, pieces):
            wa_grouped[g] = stage.tile([P, PACK * PASS], BF16, name="grouped", align_bytes=AL)
            width = PASS // pieces
            for c0 in range(0, PASS, width):
                deal(nc.scalar.copy, wa_grouped[g], wa_raw[g][:, :, c0 : c0 + width], c0 // PACK)

        h_grouped = {}

        def make_h(jh):
            rows = held([P, PACK, HALF], BF16, "h_rows%d" % jh)
            for t in range(PACK):
                acc = psum.tile([P, HALF], F32, name="acc")
                for a in range(2):
                    codes, scales = w1_q[a]
                    nc.tensor.matmul_mx(
                        out=acc[:],
                        lhsT=codes[:, P * t : P * (t + 1)].bitcast(FP8X4),
                        lhsT_scale=scales[:, P * t : P * (t + 1)],
                        rhs=v_codes(a, jh),
                        rhs_scale=v_scales(a, jh),
                        start=(a == 0),
                        stop=(a == 1),
                    )
                nc.vector.scalar_tensor_tensor(
                    out=rows[:, t, :], in0=bent[jh, t][:], scalar=gain[:, t : t + 1], in1=acc[:],
                    op0=ALU.mult, op1=ALU.add,
                )
            h_grouped[jh] = stage.tile([P, PACK * HALF], BF16, name="grouped", align_bytes=AL)
            split = HALF // 2 if jh else HALF
            interleave(nc.scalar.copy, h_grouped[jh][:, : PACK * split], rows[:, :, :split])
            if jh:
                interleave(nc.vector.tensor_copy, h_grouped[jh][:, PACK * split :], rows[:, :, split:])

        deal_wa(0, 1)
        wa_q = {0: quantise(wa_grouped[0], "wa0")}
        make_h(0)
        h_q = {0: quantise(h_grouped[0], "h0")}
        make_h(1)
        deal_wa(1, 4)

        scores = [held([P, S], F32, "e%d" % i) for i in range(8)]
        neg_top = held([P, 8], F32, "neg_top")
        tops = held([P, 2, 8], F32, "tops")

        def score(i, jh):
            g, t = divmod(i, PACK)
            acc = psum.tile([P, HALF], F32, name="acc")
            nc.tensor.matmul_mx(
                out=acc[:],
                lhsT=wa_q[g][0][:, P * t : P * (t + 1)].bitcast(FP8X4),
                lhsT_scale=wa_q[g][1][:, P * t : P * (t + 1)],
                rhs=h_q[jh][0][:].bitcast(FP8X4),
                rhs_scale=h_q[jh][1][:],
                start=True,
                stop=True,
            )
            nc.vector.tensor_scalar(
                out=scores[i][:, jh * HALF : (jh + 1) * HALF], in0=acc[:], scalar1=1.0,
                scalar2=tops[:, 0, i : i + 1] if jh else None,
                op0=ALU.mult, op1=ALU.max, accum_out=tops[:, jh, i : i + 1],
            )

        y = [held([P, PACK, M], F32, "y%d" % g) for g in range(2)]
        y_rows = out_0.rearrange("(g p t) m -> g p t m", p=P, t=PACK)
        y_scales = held([P, 2, M], U8, "y_scales")
        looked, picked, mixed = {}, {}, {}

        def look(i):
            nc.scalar.activation(
                out=neg_top[:, i : i + 1], in_=tops[:, 1, i : i + 1], func=ACT.Copy, scale=-1.0
            )
            g, t = divmod(i, PACK)
            looked[i] = ring.tile([P, M], F32, name="looked")
            nc.scalar.activation(
                out=looked[i][:], in_=scores[i][:].indirect(p1[:]), func=ACT.Exp,
                bias=neg_top[:, i : i + 1],
            )
            mixed[i] = ring.tile([P, M], F32, name="mixed")
            nc.gpsimd.tensor_tensor(
                out=mixed[i][:], in0=looked[i][:], in1=mixes[g][:, t, :], op=ALU.mult
            )

        def pick(i):
            picked[i] = ring.tile([P, M], F32, name="picked")
            nc.vector.tensor_copy(picked[i][:], scores[i][:].indirect(p2[:]))

        def finish(i):
            g, t = divmod(i, PACK)
            if i not in ON_VECTOR:
                scaled = ring.tile([P, M], F32, name="scaled")
                nc.scalar.activation(
                    out=scaled[:], in_=picked[i][:], func=ACT.Copy, scale=refs[:, g, t : t + 1]
                )
                nc.gpsimd.tensor_tensor(out=y[g][:, t, :], in0=scaled[:], in1=mixed[i][:], op=ALU.add)
            else:
                nc.vector.scalar_tensor_tensor(
                    out=y[g][:, t, :], in0=picked[i][:], scalar=refs[:, g, t : t + 1], in1=mixed[i][:],
                    op0=ALU.mult, op1=ALU.add,
                )
            nc.sync.dma_start(out=y_rows[g, :, t, :], in_=y[g][:, t, :])

        y_grouped = {}

        def group_y(g, shares):
            y_grouped[g] = stage.tile([P, PACK * M], BF16, name="grouped", align_bytes=AL)
            for copy, m0, m1 in shares:
                interleave(copy, y_grouped[g][:, PACK * m0 : PACK * m1], y[g][:, :, m0:m1])

        def planes(g):
            codes = held([P, M], U32, "y_codes%d" % g)
            nc.vector.quantize_mx(
                out=codes[:].bitcast(FP8X4), scales=y_scales[:, g, :], in_=y_grouped[g][:]
            )
            nc.sync.dma_start(
                out=out_1[g].rearrange("p m t -> p (m t)").bitcast(I32), in_=codes[:].bitcast(I32)
            )

        h_q[1] = quantise(h_grouped[1], "h1")
        score(0, 0)
        for step in range(8 + AHEAD):
            if step < 8:
                score(step, 1)
                look(step)
            if step == 0:
                score(1, 0)
            if step == 1:
                wa_q[1] = quantise(wa_grouped[1], "wa1")
            if step + 2 < 8:
                score(step + 2, 0)
            i = step - AHEAD
            if i >= 0:
                pick(i)
                if i not in ON_VECTOR:
                    finish(i)
            if step == 7:
                group_y(0, [(nc.scalar.copy, 0, M)])
        for i in ON_VECTOR:
            if i == 7:
                planes(0)
            finish(i)
        group_y(1, [(nc.vector.tensor_copy, 0, 352), (nc.scalar.copy, 352, M)])
        planes(1)
        for q in range(4):
            eng = nc.scalar if q % 2 else nc.sync
            eng.dma_start(
                out=out_2[:, 4 * q : 4 * q + 4, :].rearrange("g r m -> r g m").bitcast(I32),
                in_=y_scales[32 * q : 32 * q + 4, :, :].bitcast(I32),
            )
